import numpy as np
import ml_dtypes


def mxq(x, axis, fmt="e4m3"):
    dtype, down = {"e4m3": (ml_dtypes.float8_e4m3fn, 7), "e5m2": (ml_dtypes.float8_e5m2, 14)}[fmt]
    v = np.moveaxis(np.asarray(x, np.float32).astype(ml_dtypes.bfloat16).astype(np.float64), axis, -1)
    blocks = v.reshape(v.shape[:-1] + (-1, 32))
    amax = np.abs(blocks).max(-1, keepdims=True)
    byte = np.maximum(np.where(amax > 0, np.frexp(amax)[1] - 1 + 127, 0) - down, 1)
    scale = np.exp2(byte - 127.0)
    codes = (blocks / scale).astype(np.float32).astype(dtype).astype(np.float64)
    return np.moveaxis((codes * scale).reshape(v.shape), -1, axis)


WIDE = False


def mx_kscale(k):
    if not WIDE:
        return np.ones(k)
    levels = np.array([10, -10, 5, -5, 0])
    if k % 512:
        return np.exp2(np.random.permutation(np.resize(levels, k // 32))).repeat(32)
    a = np.empty((k // 512, 16))
    for p in range(k // 512):
        a[p, :8] = np.random.permutation(np.resize(levels, 8))
        for g in range(8):
            far = levels[np.abs(levels - a[p, g]) >= 10]
            a[p, g + 8] = far[np.random.randint(len(far))]
    return np.exp2(a.ravel()).repeat(32)


def f64(x):
    return np.asarray(x).astype(np.float64)


E2M1 = np.array([0.0, 0.5, 1.0, 1.5, 2.0, 3.0, 4.0, 6.0, -0.0, -0.5, -1.0, -1.5, -2.0, -3.0, -4.0, -6.0])


def pack_weight(w, fmt):
    k, n = w.shape
    w = f64(np.asarray(w, np.float32).astype(ml_dtypes.bfloat16)).reshape(k // 32, 32, n)
    amax = np.abs(w).max(1)
    if fmt == "e4m3":
        byte = np.frexp(amax)[1] - 1 + 127 - 7
    else:
        mant, ex = np.frexp(amax / 6.0)
        byte = np.where(mant > 0.5, ex, ex - 1) + 127
    byte = np.clip(np.where(amax > 0, byte, 1), 1, 254)
    scaled = (w * np.exp2(127.0 - byte)[:, None, :]).reshape(k, n).astype(np.float32)
    by_word = np.ascontiguousarray(scaled.reshape(k // 512, 128, 4, n).transpose(0, 1, 3, 2))
    if fmt == "e4m3":
        words = by_word.astype(ml_dtypes.float8_e4m3fn).view(np.uint8)
    else:
        c = by_word.astype(ml_dtypes.float4_e2m1fn).view(np.uint8) & 0xF
        words = (c[..., 0::2] | (c[..., 1::2] << 4)).reshape(k // 512, 128, 2 * n)
    return np.ascontiguousarray(words), np.ascontiguousarray(byte.astype(np.uint8).reshape(k // 512, 16, n))


def unpack_weight(words, scales, fmt):
    g, _, n = scales.shape
    words = np.ascontiguousarray(words).reshape(g, 128, n, -1)
    if fmt == "e4m3":
        vals = words.view(ml_dtypes.float8_e4m3fn).astype(np.float64)
    else:
        nib = np.empty((g, 128, n, 4), np.uint8)
        nib[..., 0::2] = words & 0xF
        nib[..., 1::2] = words >> 4
        vals = E2M1[nib]
    vals = vals * np.repeat(np.exp2(scales.astype(np.float64) - 127.0), 8, axis=1)[..., None]
    return vals.transpose(0, 1, 3, 2).reshape(g * 512, n)


K, T, R, N = 1024, 512, 512, 512


def setup_inputs():
    n = np.random.standard_normal
    fk = mx_kscale(K)
    fr = mx_kscale(R)
    xtp = pack_weight(n((K, T)) / fk[:, None], "e4m3")
    wap = pack_weight(n((K, R)) * 1 / np.sqrt(K) * fk[:, None] * fr, "e2m1")
    wbp = pack_weight(n((R, N)) * 1 / np.sqrt(R) / fr[:, None], "e4m3")
    wyp = pack_weight(n((K, N)) * 1 / np.sqrt(K) * fk[:, None], "e2m1")
    return {
        "xt_words": xtp[0],
        "xt_scales": xtp[1],
        "wa_words": wap[0],
        "wa_scales": wap[1],
        "dc": (np.random.uniform(0.3, 0.9, (R, 1))).astype(np.float32),
        "wb_words": wbp[0],
        "wb_scales": wbp[1],
        "wy_words": wyp[0],
        "wy_scales": wyp[1],
    }


def reference(xt_words, xt_scales, wa_words, wa_scales, dc, wb_words, wb_scales, wy_words, wy_scales):
    xtu = unpack_weight(xt_words, xt_scales, "e4m3")
    wau = unpack_weight(wa_words, wa_scales, "e2m1")
    wbu = unpack_weight(wb_words, wb_scales, "e4m3")
    wyu = unpack_weight(wy_words, wy_scales, "e2m1")
    a = wau.T @ xtu
    h1 = np.maximum(a, 0.0)
    hp = np.pad(h1, ((0, 0), (1, 0)))[:, :T]
    hid = h1 + f64(dc) * hp
    hidq = mxq(hid, 0, "e4m3")
    y = wbu.T @ hidq + wyu.T @ xtu
    return y

@@ -1,0 +1,239 @@
+from contextlib import ExitStack
+
+import concourse.mybir as mybir
+
+K, T, R, N = 1024, 512, 512, 512
+FLOPS = 2 * K * R * T + 2 * R * N * T + 2 * K * N * T
+
+F32 = mybir.dt.float32
+BF16 = mybir.dt.bfloat16
+I32 = mybir.dt.int32
+U32 = mybir.dt.uint32
+U16 = mybir.dt.uint16
+U8 = mybir.dt.uint8
+FP8X4 = mybir.dt.float8_e4m3fn_x4
+FP4X4 = mybir.dt.float4_e2m1fn_x4
+ALU = mybir.AluOpType
+
+P = 128
+PACK = 4
+KP = K // (P * PACK)
+CH = 128
+NCH = T // CH
+NT = N // P
+HALF = T // 2
+WARM = 16
+
+
+def load_scales(nc, plane, scales):
+    passes = scales.shape[0]
+    src = scales.bitcast(I32).rearrange("z (q r) c -> r q z c", r=4)
+    dst = plane[:].bitcast(I32).rearrange("p (z c) -> p z c", z=passes)
+    for r in range(4):
+        nc.sync.dma_start(out=dst[r:P:32], in_=src[r])
+
+
+def tile_mix_hidden_with_before_and_skip_kernel(
+    tc, xt_words, xt_scales, wa_words, wa_scales, dc, wb_words, wb_scales, wy_words, wy_scales, out
+):
+    nc = tc.nc
+    with ExitStack() as ctx:
+        sb = ctx.enter_context(tc.tile_pool(name="sb", bufs=1))
+        ps = ctx.enter_context(tc.psum_pool(name="ps", bufs=1))
+        ctx.enter_context(tc.manual_schedule())
+
+        wa_raw = sb.tile([P, KP * 2 * R], U8, align_bytes=64)
+        was_raw = sb.tile([P, KP * R], U8, align_bytes=64)
+        xs = sb.tile([P, KP * T], U8, align_bytes=64)
+        wys = sb.tile([P, KP * N], U8, align_bytes=64)
+        wbs = sb.tile([P, N], U8, align_bytes=64)
+        xh = [sb.tile([P, KP * HALF * PACK], U8, align_bytes=64, name="xh%d" % h) for h in range(2)]
+        wy = sb.tile([P, KP * 2 * N], U8, align_bytes=64)
+        wb = sb.tile([P, N * PACK], U8, align_bytes=64)
+        dcs = sb.tile([P, PACK], F32, align_bytes=64)
+        was = sb.tile([P, PACK * KP * P], U8, align_bytes=64)
+        wa = [sb.tile([P, KP * 2 * P], U8, align_bytes=64, name="wa%d" % j) for j in range(PACK)]
+        prev = sb.tile([P, (T + 1) * PACK], F32, align_bytes=64)
+        hid = [sb.tile([P, CH * PACK], BF16, align_bytes=64, name="hid%d" % c) for c in range(NCH)]
+        hq = [sb.tile([P, CH], U32, align_bytes=64, name="hq%d" % c) for c in range(NCH)]
+        hs = [sb.tile([P, CH], U8, align_bytes=64, name="hs%d" % c) for c in range(NCH)]
+        res = [sb.tile([P, NT * CH], F32, align_bytes=64, name="res%d" % c) for c in range(NCH - 1)]
+        res_last = [sb.tile([P, 2 * CH], F32, align_bytes=64, name="resl%d" % c) for c in range(2)]
+        zero = sb.tile([P, PACK * P], BF16, align_bytes=64)
+        zq = sb.tile([P, P], U32, align_bytes=64)
+        zs = sb.tile([P, P], U8, align_bytes=64)
+
+        ybank = [ps.tile([P, NT * CH], F32, name="y%d" % c) for c in range(NCH + 1)]
+
+        nc.vector.memset(was_raw[:].bitcast(I32), 0)
+        nc.vector.memset(xs[:].bitcast(I32), 0)
+        nc.vector.memset(zero[:], 0.0)
+        nc.vector.memset(wys[:].bitcast(I32), 0)
+        nc.vector.quantize_mx(out=zq[:].bitcast(FP8X4), scales=zs[:], in_=zero[:])
+        nc.vector.memset(wbs[:].bitcast(I32), 0)
+        nc.vector.memset(prev[:, 0:PACK], 0.0)
+
+        nc.gpsimd.dma_start(out=dcs[:], in_=dc.rearrange("(p j) o -> p (j o)", j=PACK))
+
+        x_src = xt_words.rearrange("z p t b -> p z (t b)").bitcast(I32)
+
+        def load_x(h):
+            nc.sync.dma_start(
+                out=xh[h][:].bitcast(I32).rearrange("p (z t) -> p z t", z=KP),
+                in_=x_src[:, :, h * HALF : (h + 1) * HALF],
+            )
+
+        def load_fp4(tile, words):
+            nc.sync.dma_start(
+                out=tile[:].bitcast(I32).rearrange("p (z c) -> p z c", z=KP),
+                in_=words.bitcast(I32).rearrange("z p c -> p z c"),
+            )
+
+        load_fp4(wa_raw, wa_words)
+        load_scales(nc, was_raw, wa_scales)
+        load_x(0)
+        load_scales(nc, xs, xt_scales)
+        load_x(1)
+        load_fp4(wy, wy_words)
+        load_scales(nc, wys, wy_scales)
+        nc.sync.dma_start(out=wb[:].bitcast(I32), in_=wb_words[0].rearrange("p n b -> p (n b)").bitcast(I32))
+        load_scales(nc, wbs, wb_scales)
+
+        for w in range(WARM):
+            nc.tensor.matmul_mx(
+                out=ybank[NCH][:, 0:P], lhsT=zq[:].bitcast(FP8X4), lhsT_scale=zs[:],
+                rhs=zq[:].bitcast(FP8X4), rhs_scale=zs[:], start=True, stop=True,
+            )
+
+        nc.vector.tensor_copy(
+            out=was[:].rearrange("p (j z m) -> p j z m", j=PACK, z=KP),
+            in_=was_raw[:].rearrange("p (z m j) -> p j z m", j=PACK, z=KP),
+        )
+        for j in range(PACK):
+            nc.vector.tensor_copy(
+                out=wa[j][:].bitcast(U16).rearrange("p (z m) -> p z m", z=KP),
+                in_=wa_raw[:].bitcast(U16).rearrange("p (z m j) -> p j z m", j=PACK, z=KP)[:, j],
+            )
+
+        def x_ops(c, z):
+            h, o = divmod(c * CH, HALF)
+            b0 = (z * HALF + o) * PACK
+            return (
+                xh[h][:, b0 : b0 + CH * PACK].bitcast(FP8X4),
+                xs[:, z * T + c * CH : z * T + (c + 1) * CH],
+            )
+
+        abank = {}
+
+        def first_layer(c):
+            abank[c] = ps.tile([P, PACK * CH], F32, name="a%d" % c, tag="a%d" % (c % 3))
+            for j in range(PACK):
+                for z in range(KP):
+                    xc, xsc = x_ops(c, z)
+                    s0 = (j * KP + z) * P
+                    nc.tensor.matmul_mx(
+                        out=abank[c][:, j * CH : (j + 1) * CH],
+                        lhsT=wa[j][:, z * 2 * P : (z + 1) * 2 * P].bitcast(FP4X4),
+                        lhsT_scale=was[:, s0 : s0 + P],
+                        rhs=xc, rhs_scale=xsc,
+                        start=(z == 0), stop=(z == KP - 1),
+                    )
+
+        def y_dst(c, n):
+            if c == NCH - 1:
+                b, i = divmod(n, 2)
+                return ybank[c + b][:, i * CH : (i + 1) * CH], i == 0, i == 1
+            return ybank[c][:, n * CH : (n + 1) * CH], n == 0, n == NT - 1
+
+        def skip(c):
+            for n in range(NT):
+                dst, first, last = y_dst(c, n)
+                for z in range(KP):
+                    xc, xsc = x_ops(c, z)
+                    c0 = z * N + n * P
+                    nc.tensor.matmul_mx(
+                        out=dst,
+                        lhsT=wy[:, 2 * c0 : 2 * (c0 + P)].bitcast(FP4X4),
+                        lhsT_scale=wys[:, c0 : c0 + P],
+                        rhs=xc, rhs_scale=xsc,
+                        start=(first and z == 0), stop=False,
+                    )
+
+        def second_layer(c):
+            for n in range(NT):
+                dst, first, last = y_dst(c, n)
+                nc.tensor.matmul_mx(
+                    out=dst,
+                    lhsT=wb[:, PACK * n * P : PACK * (n + 1) * P].bitcast(FP8X4),
+                    lhsT_scale=wbs[:, n * P : (n + 1) * P],
+                    rhs=hq[c][:].bitcast(FP8X4), rhs_scale=hs[c][:],
+                    start=False, stop=last,
+                )
+
+        def a_view(c):
+            return abank[c][:].rearrange("p (j t) -> p t j", j=PACK)
+
+        def carry(c):
+            o = (c * CH + 1) * PACK
+            nc.vector.scalar_tensor_tensor(
+                out=prev[:, o : o + CH * PACK].rearrange("p (t j) -> p t j", j=PACK),
+                in0=a_view(c), scalar=0.0,
+                in1=dcs[:].unsqueeze(1).broadcast_to([P, CH, PACK]),
+                op0=ALU.max, op1=ALU.mult,
+            )
+
+        def hidden(c):
+            o = c * CH * PACK
+            nc.vector.scalar_tensor_tensor(
+                out=hid[c][:].rearrange("p (t j) -> p t j", j=PACK),
+                in0=a_view(c), scalar=0.0,
+                in1=prev[:, o : o + CH * PACK].rearrange("p (t j) -> p t j", j=PACK),
+                op0=ALU.max, op1=ALU.add,
+            )
+
+        def quant(c):
+            nc.vector.quantize_mx(out=hq[c][:].bitcast(FP8X4), scales=hs[c][:], in_=hid[c][:])
+
+        out_v = out.rearrange("(n p) t -> p n t", p=P)
+
+        def store(c):
+            nc.scalar.copy(out=res[c][:], in_=ybank[c][:])
+            nc.sync.dma_start(
+                out=out_v[:, :, c * CH : (c + 1) * CH], in_=res[c][:].rearrange("p (n t) -> p n t", n=NT)
+            )
+
+        first_layer(0)
+        first_layer(1)
+        carry(0)
+        hidden(0)
+        first_layer(2)
+        carry(1)
+        quant(0)
+        hidden(1)
+        skip(0)
+        first_layer(3)
+        second_layer(0)
+        store(0)
+        carry(2)
+        quant(1)
+        hidden(2)
+        skip(1)
+        second_layer(1)
+        store(1)
+        carry(3)
+        quant(2)
+        hidden(3)
+        quant(3)
+        skip(2)
+        skip(3)
+        second_layer(2)
+        store(2)
+        second_layer(3)
+        c = NCH - 1
+        nc.scalar.copy(out=res_last[0][:], in_=ybank[c][:, 0 : 2 * CH])
+        nc.vector.tensor_copy(out=res_last[1][:], in_=ybank[c + 1][:, 0 : 2 * CH])
+        for b in range(2):
+            nc.sync.dma_start(
+                out=out_v[:, 2 * b : 2 * b + 2, c * CH : (c + 1) * CH],
+                in_=res_last[b][:].rearrange("p (n t) -> p n t", n=2),
+            )

@@ -14,6 +14,7 @@ U8 = mybir.dt.uint8
 FP8X4 = mybir.dt.float8_e4m3fn_x4
 FP4X4 = mybir.dt.float4_e2m1fn_x4
 ALU = mybir.AluOpType
+ACT = mybir.ActivationFunctionType
 
 P = 128
 PACK = 4
@@ -23,6 +24,9 @@ NCH = T // CH
 NT = N // P
 HALF = T // 2
 WARM = 16
+SCALAR_CHUNKS = (1,)
+PIECES = (2, 2, 2, 4)
+ROW = CH + 4
 
 
 def load_scales(nc, plane, scales):
@@ -53,25 +57,31 @@ def tile_mix_hidden_with_before_and_skip_kernel(
         dcs = sb.tile([P, PACK], F32, align_bytes=64)
         was = sb.tile([P, PACK * KP * P], U8, align_bytes=64)
         wa = [sb.tile([P, KP * 2 * P], U8, align_bytes=64, name="wa%d" % j) for j in range(PACK)]
-        prev = sb.tile([P, (T + 1) * PACK], F32, align_bytes=64)
+        prev_all = sb.tile([P, (T + 1) * PACK], F32, align_bytes=64)
+        prev = {}
+        relu = {}
+        for c in range(NCH):
+            if c in SCALAR_CHUNKS:
+                prev[c] = sb.tile([P, PACK, ROW], F32, align_bytes=64, name="prev%d" % c)
+                relu[c] = sb.tile([P, PACK * CH], F32, align_bytes=64, name="relu%d" % c)
+            else:
+                prev[c] = prev_all[:, c * CH * PACK : ((c + 1) * CH + 1) * PACK]
         hid = [sb.tile([P, CH * PACK], BF16, align_bytes=64, name="hid%d" % c) for c in range(NCH)]
         hq = [sb.tile([P, CH], U32, align_bytes=64, name="hq%d" % c) for c in range(NCH)]
         hs = [sb.tile([P, CH], U8, align_bytes=64, name="hs%d" % c) for c in range(NCH)]
-        res = [sb.tile([P, NT * CH], F32, align_bytes=64, name="res%d" % c) for c in range(NCH - 1)]
-        res_last = [sb.tile([P, 2 * CH], F32, align_bytes=64, name="resl%d" % c) for c in range(2)]
         zero = sb.tile([P, PACK * P], BF16, align_bytes=64)
         zq = sb.tile([P, P], U32, align_bytes=64)
         zs = sb.tile([P, P], U8, align_bytes=64)
 
-        ybank = [ps.tile([P, NT * CH], F32, name="y%d" % c) for c in range(NCH + 1)]
+        warm_bank = ps.tile([P, NT * CH], F32, name="warm_bank", tag="b7")
 
         nc.vector.memset(was_raw[:].bitcast(I32), 0)
-        nc.vector.memset(xs[:].bitcast(I32), 0)
         nc.vector.memset(zero[:], 0.0)
-        nc.vector.memset(wys[:].bitcast(I32), 0)
+        nc.vector.memset(xs[:].bitcast(I32), 0)
         nc.vector.quantize_mx(out=zq[:].bitcast(FP8X4), scales=zs[:], in_=zero[:])
+        nc.vector.memset(wys[:].bitcast(I32), 0)
         nc.vector.memset(wbs[:].bitcast(I32), 0)
-        nc.vector.memset(prev[:, 0:PACK], 0.0)
+        nc.vector.memset(prev[0][:, 0:PACK], 0.0)
 
         nc.gpsimd.dma_start(out=dcs[:], in_=dc.rearrange("(p j) o -> p (j o)", j=PACK))
 
@@ -101,7 +111,7 @@ def tile_mix_hidden_with_before_and_skip_kernel(
 
         for w in range(WARM):
             nc.tensor.matmul_mx(
-                out=ybank[NCH][:, 0:P], lhsT=zq[:].bitcast(FP8X4), lhsT_scale=zs[:],
+                out=warm_bank[:, 0:P], lhsT=zq[:].bitcast(FP8X4), lhsT_scale=zs[:],
                 rhs=zq[:].bitcast(FP8X4), rhs_scale=zs[:], start=True, stop=True,
             )
 
@@ -126,7 +136,7 @@ def tile_mix_hidden_with_before_and_skip_kernel(
         abank = {}
 
         def first_layer(c):
-            abank[c] = ps.tile([P, PACK * CH], F32, name="a%d" % c, tag="a%d" % (c % 3))
+            abank[c] = ps.tile([P, PACK * CH], F32, name="a%d" % c, tag="b%d" % c)
             for j in range(PACK):
                 for z in range(KP):
                     xc, xsc = x_ops(c, z)
@@ -139,11 +149,16 @@ def tile_mix_hidden_with_before_and_skip_kernel(
                         start=(z == 0), stop=(z == KP - 1),
                     )
 
+        ybank = {}
+
+        def open_y(c, banks):
+            for i, b in enumerate(banks):
+                ybank[c, i] = ps.tile([P, NT * CH], F32, name="y%d_%d" % (c, i), tag="b%d" % b)
+
         def y_dst(c, n):
-            if c == NCH - 1:
-                b, i = divmod(n, 2)
-                return ybank[c + b][:, i * CH : (i + 1) * CH], i == 0, i == 1
-            return ybank[c][:, n * CH : (n + 1) * CH], n == 0, n == NT - 1
+            per = NT // PIECES[c]
+            b, i = divmod(n, per)
+            return ybank[c, b][:, i * CH : (i + 1) * CH], i == 0, i == per - 1
 
         def skip(c):
             for n in range(NT):
@@ -174,21 +189,38 @@ def tile_mix_hidden_with_before_and_skip_kernel(
             return abank[c][:].rearrange("p (j t) -> p t j", j=PACK)
 
         def carry(c):
-            o = (c * CH + 1) * PACK
             nc.vector.scalar_tensor_tensor(
-                out=prev[:, o : o + CH * PACK].rearrange("p (t j) -> p t j", j=PACK),
+                out=prev[c][:, PACK:].rearrange("p (t j) -> p t j", j=PACK),
                 in0=a_view(c), scalar=0.0,
                 in1=dcs[:].unsqueeze(1).broadcast_to([P, CH, PACK]),
                 op0=ALU.max, op1=ALU.mult,
             )
 
         def hidden(c):
-            o = c * CH * PACK
             nc.vector.scalar_tensor_tensor(
                 out=hid[c][:].rearrange("p (t j) -> p t j", j=PACK),
                 in0=a_view(c), scalar=0.0,
-                in1=prev[:, o : o + CH * PACK].rearrange("p (t j) -> p t j", j=PACK),
+                in1=prev[c][:, 0 : CH * PACK].rearrange("p (t j) -> p t j", j=PACK),
                 op0=ALU.max, op1=ALU.add,
+            )
+
+        def carry_scalar(c):
+            nc.scalar.activation(out=relu[c][:], in_=abank[c][:], func=ACT.Relu)
+            nc.scalar.copy(out=prev[c][:, :, 0], in_=prev[c - 1][:, CH * PACK :])
+            for j in range(PACK):
+                nc.scalar.activation(
+                    out=prev[c][:, j, 1 : CH + 1], in_=relu[c][:, j * CH : (j + 1) * CH],
+                    func=ACT.Copy, scale=dcs[:, j : j + 1],
+                )
+            if c + 1 < NCH:
+                nc.scalar.copy(out=prev[c + 1][:, 0:PACK], in_=prev[c][:, :, CH])
+
+        def hidden_sbuf(c):
+            nc.vector.tensor_tensor(
+                out=hid[c][:].rearrange("p (u e j) -> p u j e", e=4, j=PACK),
+                in0=relu[c][:].rearrange("p (j u e) -> p u j e", e=4, j=PACK),
+                in1=prev[c][:, :, 0:CH].rearrange("p j (u e) -> p u j e", e=4),
+                op=ALU.add,
             )
 
         def quant(c):
@@ -196,44 +228,53 @@ def tile_mix_hidden_with_before_and_skip_kernel(
 
         out_v = out.rearrange("(n p) t -> p n t", p=P)
 
-        def store(c):
-            nc.scalar.copy(out=res[c][:], in_=ybank[c][:])
-            nc.sync.dma_start(
-                out=out_v[:, :, c * CH : (c + 1) * CH], in_=res[c][:].rearrange("p (n t) -> p n t", n=NT)
+        def store(c, i, on_vector=False, queue=nc.sync):
+            per = NT // PIECES[c]
+            res = sb.tile([P, per * CH], F32, align_bytes=64, name="res%d_%d" % (c, i))
+            if on_vector:
+                nc.vector.tensor_copy(out=res[:], in_=ybank[c, i][:, 0 : per * CH])
+            else:
+                nc.scalar.copy(out=res[:], in_=ybank[c, i][:, 0 : per * CH])
+            queue.dma_start(
+                out=out_v[:, i * per : (i + 1) * per, c * CH : (c + 1) * CH],
+                in_=res[:].rearrange("p (n t) -> p n t", n=per),
             )
 
         first_layer(0)
         first_layer(1)
+        first_layer(2)
+        first_layer(3)
         carry(0)
         hidden(0)
-        first_layer(2)
-        carry(1)
-        quant(0)
-        hidden(1)
-        skip(0)
-        first_layer(3)
-        second_layer(0)
-        store(0)
+        carry_scalar(1)
         carry(2)
-        quant(1)
+        quant(0)
+        hidden_sbuf(1)
+        open_y(0, (4, 5))
+        skip(0)
+        second_layer(0)
+        store(0, 0)
+        store(0, 1)
         hidden(2)
+        quant(1)
+        open_y(1, (6, 7))
         skip(1)
         second_layer(1)
-        store(1)
+        store(1, 0)
+        store(1, 1)
         carry(3)
         quant(2)
         hidden(3)
         quant(3)
+        open_y(2, (0, 1))
         skip(2)
-        skip(3)
         second_layer(2)
-        store(2)
+        store(2, 0)
+        store(2, 1)
+        open_y(3, (2, 4, 5, 6))
+        skip(3)
         second_layer(3)
-        c = NCH - 1
-        nc.scalar.copy(out=res_last[0][:], in_=ybank[c][:, 0 : 2 * CH])
-        nc.vector.tensor_copy(out=res_last[1][:], in_=ybank[c + 1][:, 0 : 2 * CH])
-        for b in range(2):
-            nc.sync.dma_start(
-                out=out_v[:, 2 * b : 2 * b + 2, c * CH : (c + 1) * CH],
-                in_=res_last[b][:].rearrange("p (n t) -> p n t", n=2),
-            )
+        store(3, 0, False, nc.scalar)
+        store(3, 1, True)
+        store(3, 2, False, nc.scalar)
+        store(3, 3, True)

@@ -46,32 +46,32 @@ def tile_mix_hidden_with_before_and_skip_kernel(
         ps = ctx.enter_context(tc.psum_pool(name="ps", bufs=1))
         ctx.enter_context(tc.manual_schedule())
 
-        wa_raw = sb.tile([P, KP * 2 * R], U8, align_bytes=64)
-        was_raw = sb.tile([P, KP * R], U8, align_bytes=64)
-        xs = sb.tile([P, KP * T], U8, align_bytes=64)
-        wys = sb.tile([P, KP * N], U8, align_bytes=64)
-        wbs = sb.tile([P, N], U8, align_bytes=64)
-        xh = [sb.tile([P, KP * HALF * PACK], U8, align_bytes=64, name="xh%d" % h) for h in range(2)]
-        wy = sb.tile([P, KP * 2 * N], U8, align_bytes=64)
-        wb = sb.tile([P, N * PACK], U8, align_bytes=64)
-        dcs = sb.tile([P, PACK], F32, align_bytes=64)
-        was = sb.tile([P, PACK * KP * P], U8, align_bytes=64)
-        wa = [sb.tile([P, KP * 2 * P], U8, align_bytes=64, name="wa%d" % j) for j in range(PACK)]
-        prev_all = sb.tile([P, (T + 1) * PACK], F32, align_bytes=64)
+        wa_raw = sb.tile([P, KP * 2 * R], U8, align_bytes=256)
+        was_raw = sb.tile([P, KP * R], U8, align_bytes=256)
+        xs = sb.tile([P, KP * T], U8, align_bytes=256)
+        wys = sb.tile([P, KP * N], U8, align_bytes=256)
+        wbs = sb.tile([P, N], U8, align_bytes=256)
+        xh = [sb.tile([P, KP * HALF * PACK], U8, align_bytes=256, name="xh%d" % h) for h in range(2)]
+        wy = sb.tile([P, KP * 2 * N], U8, align_bytes=256)
+        wb = sb.tile([P, N * PACK], U8, align_bytes=256)
+        dcs = sb.tile([P, PACK], F32, align_bytes=256)
+        was = sb.tile([P, PACK * KP * P], U8, align_bytes=256)
+        wa = [sb.tile([P, KP * 2 * P], U8, align_bytes=256, name="wa%d" % j) for j in range(PACK)]
+        prev_all = sb.tile([P, (T + 1) * PACK], F32, align_bytes=256)
         prev = {}
         relu = {}
         for c in range(NCH):
             if c in SCALAR_CHUNKS:
-                prev[c] = sb.tile([P, PACK, ROW], F32, align_bytes=64, name="prev%d" % c)
-                relu[c] = sb.tile([P, PACK * CH], F32, align_bytes=64, name="relu%d" % c)
+                prev[c] = sb.tile([P, PACK, ROW], F32, align_bytes=256, name="prev%d" % c)
+                relu[c] = sb.tile([P, PACK * CH], F32, align_bytes=256, name="relu%d" % c)
             else:
                 prev[c] = prev_all[:, c * CH * PACK : ((c + 1) * CH + 1) * PACK]
-        hid = [sb.tile([P, CH * PACK], BF16, align_bytes=64, name="hid%d" % c) for c in range(NCH)]
-        hq = [sb.tile([P, CH], U32, align_bytes=64, name="hq%d" % c) for c in range(NCH)]
-        hs = [sb.tile([P, CH], U8, align_bytes=64, name="hs%d" % c) for c in range(NCH)]
-        zero = sb.tile([P, PACK * P], BF16, align_bytes=64)
-        zq = sb.tile([P, P], U32, align_bytes=64)
-        zs = sb.tile([P, P], U8, align_bytes=64)
+        hid = [sb.tile([P, CH * PACK], BF16, align_bytes=256, name="hid%d" % c) for c in range(NCH)]
+        hq = [sb.tile([P, CH], U32, align_bytes=256, name="hq%d" % c) for c in range(NCH)]
+        hs = [sb.tile([P, CH], U8, align_bytes=256, name="hs%d" % c) for c in range(NCH)]
+        zero = sb.tile([P, PACK * P], BF16, align_bytes=256)
+        zq = sb.tile([P, P], U32, align_bytes=256)
+        zs = sb.tile([P, P], U8, align_bytes=256)
 
         warm_bank = ps.tile([P, NT * CH], F32, name="warm_bank", tag="b7")
 
@@ -83,7 +83,6 @@ def tile_mix_hidden_with_before_and_skip_kernel(
         nc.vector.memset(wbs[:].bitcast(I32), 0)
         nc.vector.memset(prev[0][:, 0:PACK], 0.0)
 
-        nc.gpsimd.dma_start(out=dcs[:], in_=dc.rearrange("(p j) o -> p (j o)", j=PACK))
 
         x_src = xt_words.rearrange("z p t b -> p z (t b)").bitcast(I32)
 
@@ -104,6 +103,7 @@ def tile_mix_hidden_with_before_and_skip_kernel(
         load_x(0)
         load_scales(nc, xs, xt_scales)
         load_x(1)
+        nc.sync.dma_start(out=dcs[:], in_=dc.rearrange("(p j) o -> p (j o)", j=PACK))
         load_fp4(wy, wy_words)
         load_scales(nc, wys, wy_scales)
         nc.sync.dma_start(out=wb[:].bitcast(I32), in_=wb_words[0].rearrange("p n b -> p (n b)").bitcast(I32))
@@ -115,14 +115,16 @@ def tile_mix_hidden_with_before_and_skip_kernel(
                 rhs=zq[:].bitcast(FP8X4), rhs_scale=zs[:], start=True, stop=True,
             )
 
-        nc.vector.tensor_copy(
-            out=was[:].rearrange("p (j z m) -> p j z m", j=PACK, z=KP),
-            in_=was_raw[:].rearrange("p (z m j) -> p j z m", j=PACK, z=KP),
-        )
         for j in range(PACK):
             nc.vector.tensor_copy(
                 out=wa[j][:].bitcast(U16).rearrange("p (z m) -> p z m", z=KP),
                 in_=wa_raw[:].bitcast(U16).rearrange("p (z m j) -> p j z m", j=PACK, z=KP)[:, j],
+            )
+
+        for j in range(0, PACK, 2):
+            nc.vector.tensor_copy(
+                out=was[:].rearrange("p (j z m) -> p j z m", j=PACK, z=KP)[:, j : j + 2],
+                in_=was_raw[:].rearrange("p (z m j) -> p j z m", j=PACK, z=KP)[:, j : j + 2],
             )
 
         def x_ops(c, z):
@@ -217,9 +219,9 @@ def tile_mix_hidden_with_before_and_skip_kernel(
 
         def hidden_sbuf(c):
             nc.vector.tensor_tensor(
-                out=hid[c][:].rearrange("p (u e j) -> p u j e", e=4, j=PACK),
-                in0=relu[c][:].rearrange("p (j u e) -> p u j e", e=4, j=PACK),
-                in1=prev[c][:, :, 0:CH].rearrange("p j (u e) -> p u j e", e=4),
+                out=hid[c][:].rearrange("p (u e j) -> p u j e", e=2, j=PACK),
+                in0=relu[c][:].rearrange("p (j u e) -> p u j e", e=2, j=PACK),
+                in1=prev[c][:, :, 0:CH].rearrange("p j (u e) -> p u j e", e=2),
                 op=ALU.add,
             )
 
@@ -230,7 +232,7 @@ def tile_mix_hidden_with_before_and_skip_kernel(
 
         def store(c, i, on_vector=False, queue=nc.sync):
             per = NT // PIECES[c]
-            res = sb.tile([P, per * CH], F32, align_bytes=64, name="res%d_%d" % (c, i))
+            res = sb.tile([P, per * CH], F32, align_bytes=256, name="res%d_%d" % (c, i))
             if on_vector:
                 nc.vector.tensor_copy(out=res[:], in_=ybank[c, i][:, 0 : per * CH])
             else:

@@ -18,23 +18,33 @@ ACT = mybir.ActivationFunctionType
 
 P = 128
 PACK = 4
-KP = K // (P * PACK)
-CH = 128
-NCH = T // CH
-NT = N // P
+FP4_BYTES = 2
+QUADRANT = 32
+SCALE_ROWS = 4
+K_PASSES = K // (P * PACK)
+CHUNK = 128
+CHUNKS = T // CHUNK
+N_TILES = N // P
 HALF = T // 2
-WARM = 16
-SCALAR_CHUNKS = (1,)
-PIECES = (2, 2, 2, 4)
-ROW = CH + 4
+ALIGN = 256
+WARM_PASSES = 16
+SCALAR_CHUNK = 1
+CARRY_ROW = CHUNK + 4
+PAIR = 2
 
 
 def load_scales(nc, plane, scales):
-    passes = scales.shape[0]
-    src = scales.bitcast(I32).rearrange("z (q r) c -> r q z c", r=4)
-    dst = plane[:].bitcast(I32).rearrange("p (z c) -> p z c", z=passes)
-    for r in range(4):
-        nc.sync.dma_start(out=dst[r:P:32], in_=src[r])
+    src = scales.bitcast(I32).rearrange("z (q i) c -> i q z c", i=SCALE_ROWS)
+    dst = plane[:].bitcast(I32).rearrange("p (z c) -> p z c", z=scales.shape[0])
+    for i in range(SCALE_ROWS):
+        nc.sync.dma_start(out=dst[i:P:QUADRANT], in_=src[i])
+
+
+def load_fp4(nc, tile, words):
+    nc.sync.dma_start(
+        out=tile[:].bitcast(I32).rearrange("p (z c) -> p z c", z=K_PASSES),
+        in_=words.bitcast(I32).rearrange("z p c -> p z c"),
+    )
 
 
 def tile_mix_hidden_with_before_and_skip_kernel(
@@ -46,237 +56,201 @@ def tile_mix_hidden_with_before_and_skip_kernel(
         ps = ctx.enter_context(tc.psum_pool(name="ps", bufs=1))
         ctx.enter_context(tc.manual_schedule())
 
-        wa_raw = sb.tile([P, KP * 2 * R], U8, align_bytes=256)
-        was_raw = sb.tile([P, KP * R], U8, align_bytes=256)
-        xs = sb.tile([P, KP * T], U8, align_bytes=256)
-        wys = sb.tile([P, KP * N], U8, align_bytes=256)
-        wbs = sb.tile([P, N], U8, align_bytes=256)
-        xh = [sb.tile([P, KP * HALF * PACK], U8, align_bytes=256, name="xh%d" % h) for h in range(2)]
-        wy = sb.tile([P, KP * 2 * N], U8, align_bytes=256)
-        wb = sb.tile([P, N * PACK], U8, align_bytes=256)
-        dcs = sb.tile([P, PACK], F32, align_bytes=256)
-        was = sb.tile([P, PACK * KP * P], U8, align_bytes=256)
-        wa = [sb.tile([P, KP * 2 * P], U8, align_bytes=256, name="wa%d" % j) for j in range(PACK)]
-        prev_all = sb.tile([P, (T + 1) * PACK], F32, align_bytes=256)
-        prev = {}
-        relu = {}
-        for c in range(NCH):
-            if c in SCALAR_CHUNKS:
-                prev[c] = sb.tile([P, PACK, ROW], F32, align_bytes=256, name="prev%d" % c)
-                relu[c] = sb.tile([P, PACK * CH], F32, align_bytes=256, name="relu%d" % c)
-            else:
-                prev[c] = prev_all[:, c * CH * PACK : ((c + 1) * CH + 1) * PACK]
-        hid = [sb.tile([P, CH * PACK], BF16, align_bytes=256, name="hid%d" % c) for c in range(NCH)]
-        hq = [sb.tile([P, CH], U32, align_bytes=256, name="hq%d" % c) for c in range(NCH)]
-        hs = [sb.tile([P, CH], U8, align_bytes=256, name="hs%d" % c) for c in range(NCH)]
-        zero = sb.tile([P, PACK * P], BF16, align_bytes=256)
-        zq = sb.tile([P, P], U32, align_bytes=256)
-        zs = sb.tile([P, P], U8, align_bytes=256)
+        wa_raw = sb.tile([P, K_PASSES * FP4_BYTES * R], U8, align_bytes=ALIGN)
+        wa_plane_raw = sb.tile([P, K_PASSES * R], U8, align_bytes=ALIGN)
+        x_plane = sb.tile([P, K_PASSES * T], U8, align_bytes=ALIGN)
+        wy_plane = sb.tile([P, K_PASSES * N], U8, align_bytes=ALIGN)
+        wb_plane = sb.tile([P, N], U8, align_bytes=ALIGN)
+        x_half = [sb.tile([P, K_PASSES * HALF * PACK], U8, align_bytes=ALIGN, name="x_half%d" % h) for h in range(2)]
+        wy = sb.tile([P, K_PASSES * FP4_BYTES * N], U8, align_bytes=ALIGN)
+        wb = sb.tile([P, N * PACK], U8, align_bytes=ALIGN)
+        factor = sb.tile([P, PACK], F32, align_bytes=ALIGN)
+        wa_plane = sb.tile([P, PACK * K_PASSES * P], U8, align_bytes=ALIGN)
+        wa = [sb.tile([P, K_PASSES * FP4_BYTES * P], U8, align_bytes=ALIGN, name="wa%d" % j) for j in range(PACK)]
+        carried = sb.tile([P, (T + 1) * PACK], F32, align_bytes=ALIGN)
+        carried_rows = sb.tile([P, PACK, CARRY_ROW], F32, align_bytes=ALIGN)
+        relu_rows = sb.tile([P, PACK * CHUNK], F32, align_bytes=ALIGN)
+        hid = [sb.tile([P, CHUNK * PACK], BF16, align_bytes=ALIGN, name="hid%d" % c) for c in range(CHUNKS)]
+        hid_codes = [sb.tile([P, CHUNK], U32, align_bytes=ALIGN, name="hid_codes%d" % c) for c in range(CHUNKS)]
+        hid_plane = [sb.tile([P, CHUNK], U8, align_bytes=ALIGN, name="hid_plane%d" % c) for c in range(CHUNKS)]
+        zero = sb.tile([P, PACK * P], BF16, align_bytes=ALIGN)
+        zero_codes = sb.tile([P, P], U32, align_bytes=ALIGN)
+        zero_plane = sb.tile([P, P], U8, align_bytes=ALIGN)
 
-        warm_bank = ps.tile([P, NT * CH], F32, name="warm_bank", tag="b7")
+        def bank(name, index):
+            return ps.tile([P, N_TILES * CHUNK], F32, name=name, tag="bank%d" % index)
 
-        nc.vector.memset(was_raw[:].bitcast(I32), 0)
+        warm_bank = bank("warm_bank", 7)
+
+        nc.vector.memset(wa_plane_raw[:].bitcast(I32), 0)
         nc.vector.memset(zero[:], 0.0)
-        nc.vector.memset(xs[:].bitcast(I32), 0)
-        nc.vector.quantize_mx(out=zq[:].bitcast(FP8X4), scales=zs[:], in_=zero[:])
-        nc.vector.memset(wys[:].bitcast(I32), 0)
-        nc.vector.memset(wbs[:].bitcast(I32), 0)
-        nc.vector.memset(prev[0][:, 0:PACK], 0.0)
-
+        nc.vector.memset(x_plane[:].bitcast(I32), 0)
+        nc.vector.quantize_mx(out=zero_codes[:].bitcast(FP8X4), scales=zero_plane[:], in_=zero[:])
+        nc.vector.memset(wy_plane[:].bitcast(I32), 0)
+        nc.vector.memset(wb_plane[:].bitcast(I32), 0)
+        nc.vector.memset(carried[:, 0:PACK], 0.0)
 
         x_src = xt_words.rearrange("z p t b -> p z (t b)").bitcast(I32)
 
         def load_x(h):
             nc.sync.dma_start(
-                out=xh[h][:].bitcast(I32).rearrange("p (z t) -> p z t", z=KP),
+                out=x_half[h][:].bitcast(I32).rearrange("p (z t) -> p z t", z=K_PASSES),
                 in_=x_src[:, :, h * HALF : (h + 1) * HALF],
             )
 
-        def load_fp4(tile, words):
-            nc.sync.dma_start(
-                out=tile[:].bitcast(I32).rearrange("p (z c) -> p z c", z=KP),
-                in_=words.bitcast(I32).rearrange("z p c -> p z c"),
-            )
-
-        load_fp4(wa_raw, wa_words)
-        load_scales(nc, was_raw, wa_scales)
+        load_fp4(nc, wa_raw, wa_words)
+        load_scales(nc, wa_plane_raw, wa_scales)
         load_x(0)
-        load_scales(nc, xs, xt_scales)
+        load_scales(nc, x_plane, xt_scales)
+        nc.sync.dma_start(out=factor[:], in_=dc.rearrange("(p j) o -> p (j o)", j=PACK))
         load_x(1)
-        nc.sync.dma_start(out=dcs[:], in_=dc.rearrange("(p j) o -> p (j o)", j=PACK))
-        load_fp4(wy, wy_words)
-        load_scales(nc, wys, wy_scales)
+        load_scales(nc, wy_plane, wy_scales)
+        load_fp4(nc, wy, wy_words)
         nc.sync.dma_start(out=wb[:].bitcast(I32), in_=wb_words[0].rearrange("p n b -> p (n b)").bitcast(I32))
-        load_scales(nc, wbs, wb_scales)
+        load_scales(nc, wb_plane, wb_scales)
 
-        for w in range(WARM):
+        for w in range(WARM_PASSES):
             nc.tensor.matmul_mx(
-                out=warm_bank[:, 0:P], lhsT=zq[:].bitcast(FP8X4), lhsT_scale=zs[:],
-                rhs=zq[:].bitcast(FP8X4), rhs_scale=zs[:], start=True, stop=True,
+                out=warm_bank[:, 0:P], lhsT=zero_codes[:].bitcast(FP8X4), lhsT_scale=zero_plane[:],
+                rhs=zero_codes[:].bitcast(FP8X4), rhs_scale=zero_plane[:], start=True, stop=True,
             )
 
         for j in range(PACK):
             nc.vector.tensor_copy(
-                out=wa[j][:].bitcast(U16).rearrange("p (z m) -> p z m", z=KP),
-                in_=wa_raw[:].bitcast(U16).rearrange("p (z m j) -> p j z m", j=PACK, z=KP)[:, j],
+                out=wa[j][:].bitcast(U16).rearrange("p (z m) -> p z m", z=K_PASSES),
+                in_=wa_raw[:].bitcast(U16).rearrange("p (z m j) -> p j z m", j=PACK, z=K_PASSES)[:, j],
             )
-
         for j in range(0, PACK, 2):
             nc.vector.tensor_copy(
-                out=was[:].rearrange("p (j z m) -> p j z m", j=PACK, z=KP)[:, j : j + 2],
-                in_=was_raw[:].rearrange("p (z m j) -> p j z m", j=PACK, z=KP)[:, j : j + 2],
+                out=wa_plane[:].rearrange("p (j z m) -> p j z m", j=PACK, z=K_PASSES)[:, j : j + 2],
+                in_=wa_plane_raw[:].rearrange("p (z m j) -> p j z m", j=PACK, z=K_PASSES)[:, j : j + 2],
             )
 
-        def x_ops(c, z):
-            h, o = divmod(c * CH, HALF)
-            b0 = (z * HALF + o) * PACK
-            return (
-                xh[h][:, b0 : b0 + CH * PACK].bitcast(FP8X4),
-                xs[:, z * T + c * CH : z * T + (c + 1) * CH],
-            )
-
-        abank = {}
+        def x_operand(c, z):
+            h, first = divmod(c * CHUNK, HALF)
+            byte = (z * HALF + first) * PACK
+            column = z * T + c * CHUNK
+            return x_half[h][:, byte : byte + CHUNK * PACK].bitcast(FP8X4), x_plane[:, column : column + CHUNK]
 
         def first_layer(c):
-            abank[c] = ps.tile([P, PACK * CH], F32, name="a%d" % c, tag="b%d" % c)
+            a = bank("a%d" % c, c)
             for j in range(PACK):
-                for z in range(KP):
-                    xc, xsc = x_ops(c, z)
-                    s0 = (j * KP + z) * P
+                for z in range(K_PASSES):
+                    x_codes, x_scales = x_operand(c, z)
+                    column = (j * K_PASSES + z) * P
                     nc.tensor.matmul_mx(
-                        out=abank[c][:, j * CH : (j + 1) * CH],
-                        lhsT=wa[j][:, z * 2 * P : (z + 1) * 2 * P].bitcast(FP4X4),
-                        lhsT_scale=was[:, s0 : s0 + P],
-                        rhs=xc, rhs_scale=xsc,
-                        start=(z == 0), stop=(z == KP - 1),
+                        out=a[:, j * CHUNK : (j + 1) * CHUNK],
+                        lhsT=wa[j][:, z * FP4_BYTES * P : (z + 1) * FP4_BYTES * P].bitcast(FP4X4),
+                        lhsT_scale=wa_plane[:, column : column + P],
+                        rhs=x_codes, rhs_scale=x_scales,
+                        start=(z == 0), stop=(z == K_PASSES - 1),
                     )
+            return a
 
-        ybank = {}
+        a_bank = [first_layer(c) for c in range(CHUNKS)]
 
-        def open_y(c, banks):
-            for i, b in enumerate(banks):
-                ybank[c, i] = ps.tile([P, NT * CH], F32, name="y%d_%d" % (c, i), tag="b%d" % b)
+        def slots(first, count):
+            return carried[:, first * PACK : (first + count) * PACK]
 
-        def y_dst(c, n):
-            per = NT // PIECES[c]
-            b, i = divmod(n, per)
-            return ybank[c, b][:, i * CH : (i + 1) * CH], i == 0, i == per - 1
-
-        def skip(c):
-            for n in range(NT):
-                dst, first, last = y_dst(c, n)
-                for z in range(KP):
-                    xc, xsc = x_ops(c, z)
-                    c0 = z * N + n * P
-                    nc.tensor.matmul_mx(
-                        out=dst,
-                        lhsT=wy[:, 2 * c0 : 2 * (c0 + P)].bitcast(FP4X4),
-                        lhsT_scale=wys[:, c0 : c0 + P],
-                        rhs=xc, rhs_scale=xsc,
-                        start=(first and z == 0), stop=False,
-                    )
-
-        def second_layer(c):
-            for n in range(NT):
-                dst, first, last = y_dst(c, n)
-                nc.tensor.matmul_mx(
-                    out=dst,
-                    lhsT=wb[:, PACK * n * P : PACK * (n + 1) * P].bitcast(FP8X4),
-                    lhsT_scale=wbs[:, n * P : (n + 1) * P],
-                    rhs=hq[c][:].bitcast(FP8X4), rhs_scale=hs[c][:],
-                    start=False, stop=last,
-                )
-
-        def a_view(c):
-            return abank[c][:].rearrange("p (j t) -> p t j", j=PACK)
-
-        def carry(c):
+        def carry_on_vector(c):
             nc.vector.scalar_tensor_tensor(
-                out=prev[c][:, PACK:].rearrange("p (t j) -> p t j", j=PACK),
-                in0=a_view(c), scalar=0.0,
-                in1=dcs[:].unsqueeze(1).broadcast_to([P, CH, PACK]),
+                out=slots(c * CHUNK + 1, CHUNK).rearrange("p (t j) -> p t j", j=PACK),
+                in0=a_bank[c][:].rearrange("p (j t) -> p t j", j=PACK), scalar=0.0,
+                in1=factor[:].unsqueeze(1).broadcast_to([P, CHUNK, PACK]),
                 op0=ALU.max, op1=ALU.mult,
             )
 
-        def hidden(c):
+        def hidden_from_bank(c):
             nc.vector.scalar_tensor_tensor(
                 out=hid[c][:].rearrange("p (t j) -> p t j", j=PACK),
-                in0=a_view(c), scalar=0.0,
-                in1=prev[c][:, 0 : CH * PACK].rearrange("p (t j) -> p t j", j=PACK),
+                in0=a_bank[c][:].rearrange("p (j t) -> p t j", j=PACK), scalar=0.0,
+                in1=slots(c * CHUNK, CHUNK).rearrange("p (t j) -> p t j", j=PACK),
                 op0=ALU.max, op1=ALU.add,
             )
 
-        def carry_scalar(c):
-            nc.scalar.activation(out=relu[c][:], in_=abank[c][:], func=ACT.Relu)
-            nc.scalar.copy(out=prev[c][:, :, 0], in_=prev[c - 1][:, CH * PACK :])
+        def carry_on_scalar(c):
+            nc.scalar.activation(out=relu_rows[:], in_=a_bank[c][:], func=ACT.Relu)
+            nc.scalar.copy(out=carried_rows[:, :, 0], in_=slots(c * CHUNK, 1))
             for j in range(PACK):
                 nc.scalar.activation(
-                    out=prev[c][:, j, 1 : CH + 1], in_=relu[c][:, j * CH : (j + 1) * CH],
-                    func=ACT.Copy, scale=dcs[:, j : j + 1],
+                    out=carried_rows[:, j, 1 : CHUNK + 1], in_=relu_rows[:, j * CHUNK : (j + 1) * CHUNK],
+                    func=ACT.Copy, scale=factor[:, j : j + 1],
                 )
-            if c + 1 < NCH:
-                nc.scalar.copy(out=prev[c + 1][:, 0:PACK], in_=prev[c][:, :, CH])
+            nc.scalar.copy(out=slots((c + 1) * CHUNK, 1), in_=carried_rows[:, :, CHUNK])
 
-        def hidden_sbuf(c):
+        def hidden_from_rows(c):
             nc.vector.tensor_tensor(
-                out=hid[c][:].rearrange("p (u e j) -> p u j e", e=2, j=PACK),
-                in0=relu[c][:].rearrange("p (j u e) -> p u j e", e=2, j=PACK),
-                in1=prev[c][:, :, 0:CH].rearrange("p j (u e) -> p u j e", e=2),
+                out=hid[c][:].rearrange("p (u e j) -> p u j e", e=PAIR, j=PACK),
+                in0=relu_rows[:].rearrange("p (j u e) -> p u j e", e=PAIR, j=PACK),
+                in1=carried_rows[:, :, 0:CHUNK].rearrange("p j (u e) -> p u j e", e=PAIR),
                 op=ALU.add,
             )
 
-        def quant(c):
-            nc.vector.quantize_mx(out=hq[c][:].bitcast(FP8X4), scales=hs[c][:], in_=hid[c][:])
+        def quantize(c):
+            nc.vector.quantize_mx(out=hid_codes[c][:].bitcast(FP8X4), scales=hid_plane[c][:], in_=hid[c][:])
 
-        out_v = out.rearrange("(n p) t -> p n t", p=P)
+        out_tiles = out.rearrange("(n p) t -> p n t", p=P)
 
-        def store(c, i, on_vector=False, queue=nc.sync):
-            per = NT // PIECES[c]
-            res = sb.tile([P, per * CH], F32, align_bytes=256, name="res%d_%d" % (c, i))
-            if on_vector:
-                nc.vector.tensor_copy(out=res[:], in_=ybank[c, i][:, 0 : per * CH])
-            else:
-                nc.scalar.copy(out=res[:], in_=ybank[c, i][:, 0 : per * CH])
+        def products(c, banks):
+            per_bank = N_TILES // len(banks)
+            y = [bank("y%d_%d" % (c, i), index) for i, index in enumerate(banks)]
+            for n in range(N_TILES):
+                i, place = divmod(n, per_bank)
+                for z in range(K_PASSES):
+                    x_codes, x_scales = x_operand(c, z)
+                    column = z * N + n * P
+                    nc.tensor.matmul_mx(
+                        out=y[i][:, place * CHUNK : (place + 1) * CHUNK],
+                        lhsT=wy[:, FP4_BYTES * column : FP4_BYTES * (column + P)].bitcast(FP4X4),
+                        lhsT_scale=wy_plane[:, column : column + P],
+                        rhs=x_codes, rhs_scale=x_scales,
+                        start=(place == 0 and z == 0), stop=False,
+                    )
+            for n in range(N_TILES):
+                i, place = divmod(n, per_bank)
+                nc.tensor.matmul_mx(
+                    out=y[i][:, place * CHUNK : (place + 1) * CHUNK],
+                    lhsT=wb[:, PACK * n * P : PACK * (n + 1) * P].bitcast(FP8X4),
+                    lhsT_scale=wb_plane[:, n * P : (n + 1) * P],
+                    rhs=hid_codes[c][:].bitcast(FP8X4), rhs_scale=hid_plane[c][:],
+                    start=False, stop=(place == per_bank - 1),
+                )
+            return y
+
+        def store(c, y, i, copy, queue):
+            per_bank = N_TILES // len(y)
+            result = sb.tile([P, per_bank * CHUNK], F32, align_bytes=ALIGN, name="result%d_%d" % (c, i))
+            copy(out=result[:], in_=y[i][:, 0 : per_bank * CHUNK])
             queue.dma_start(
-                out=out_v[:, i * per : (i + 1) * per, c * CH : (c + 1) * CH],
-                in_=res[:].rearrange("p (n t) -> p n t", n=per),
+                out=out_tiles[:, i * per_bank : (i + 1) * per_bank, c * CHUNK : (c + 1) * CHUNK],
+                in_=result[:].rearrange("p (n t) -> p n t", n=per_bank),
             )
 
-        first_layer(0)
-        first_layer(1)
-        first_layer(2)
-        first_layer(3)
-        carry(0)
-        hidden(0)
-        carry_scalar(1)
-        carry(2)
-        quant(0)
-        hidden_sbuf(1)
-        open_y(0, (4, 5))
-        skip(0)
-        second_layer(0)
-        store(0, 0)
-        store(0, 1)
-        hidden(2)
-        quant(1)
-        open_y(1, (6, 7))
-        skip(1)
-        second_layer(1)
-        store(1, 0)
-        store(1, 1)
-        carry(3)
-        quant(2)
-        hidden(3)
-        quant(3)
-        open_y(2, (0, 1))
-        skip(2)
-        second_layer(2)
-        store(2, 0)
-        store(2, 1)
-        open_y(3, (2, 4, 5, 6))
-        skip(3)
-        second_layer(3)
-        store(3, 0, False, nc.scalar)
-        store(3, 1, True)
-        store(3, 2, False, nc.scalar)
-        store(3, 3, True)
+        def finish_in_halves(c, banks):
+            y = products(c, banks)
+            for i in range(len(y)):
+                store(c, y, i, nc.scalar.copy, nc.sync)
+
+        carry_on_vector(0)
+        hidden_from_bank(0)
+        carry_on_scalar(SCALAR_CHUNK)
+        carry_on_vector(2)
+        quantize(0)
+        hidden_from_rows(SCALAR_CHUNK)
+        finish_in_halves(0, (4, 5))
+        hidden_from_bank(2)
+        quantize(1)
+        finish_in_halves(1, (6, 7))
+        carry_on_vector(3)
+        quantize(2)
+        hidden_from_bank(3)
+        quantize(3)
+        finish_in_halves(2, (0, 1))
+
+        last = CHUNKS - 1
+        y_last = products(last, (2, 4, 5, 6))
+        for i in range(N_TILES):
+            if i % 2 == 0:
+                store(last, y_last, i, nc.scalar.copy, nc.scalar)
+            else:
+                store(last, y_last, i, nc.vector.tensor_copy, nc.sync)

from contextlib import ExitStack

import concourse.mybir as mybir

K, T, R, N = 1024, 512, 512, 512
FLOPS = 2 * K * R * T + 2 * R * N * T + 2 * K * N * T

F32 = mybir.dt.float32
BF16 = mybir.dt.bfloat16
I32 = mybir.dt.int32
U32 = mybir.dt.uint32
U16 = mybir.dt.uint16
U8 = mybir.dt.uint8
FP8X4 = mybir.dt.float8_e4m3fn_x4
FP4X4 = mybir.dt.float4_e2m1fn_x4
ALU = mybir.AluOpType
ACT = mybir.ActivationFunctionType

P = 128
PACK = 4
FP4_BYTES = 2
QUADRANT = 32
SCALE_ROWS = 4
K_PASSES = K // (P * PACK)
CHUNK = 128
CHUNKS = T // CHUNK
N_TILES = N // P
HALF = T // 2
ALIGN = 256
WARM_PASSES = 16
SCALAR_CHUNK = 1
CARRY_ROW = CHUNK + 4
PAIR = 2


def load_scales(nc, plane, scales):
    src = scales.bitcast(I32).rearrange("z (q i) c -> i q z c", i=SCALE_ROWS)
    dst = plane[:].bitcast(I32).rearrange("p (z c) -> p z c", z=scales.shape[0])
    for i in range(SCALE_ROWS):
        nc.sync.dma_start(out=dst[i:P:QUADRANT], in_=src[i])


def load_fp4(nc, tile, words):
    nc.sync.dma_start(
        out=tile[:].bitcast(I32).rearrange("p (z c) -> p z c", z=K_PASSES),
        in_=words.bitcast(I32).rearrange("z p c -> p z c"),
    )


def tile_mix_hidden_with_before_and_skip_kernel(
    tc, xt_words, xt_scales, wa_words, wa_scales, dc, wb_words, wb_scales, wy_words, wy_scales, out
):
    nc = tc.nc
    with ExitStack() as ctx:
        sb = ctx.enter_context(tc.tile_pool(name="sb", bufs=1))
        ps = ctx.enter_context(tc.psum_pool(name="ps", bufs=1))
        ctx.enter_context(tc.manual_schedule())

        wa_raw = sb.tile([P, K_PASSES * FP4_BYTES * R], U8, align_bytes=ALIGN)
        wa_plane_raw = sb.tile([P, K_PASSES * R], U8, align_bytes=ALIGN)
        x_plane = sb.tile([P, K_PASSES * T], U8, align_bytes=ALIGN)
        wy_plane = sb.tile([P, K_PASSES * N], U8, align_bytes=ALIGN)
        wb_plane = sb.tile([P, N], U8, align_bytes=ALIGN)
        x_half = [sb.tile([P, K_PASSES * HALF * PACK], U8, align_bytes=ALIGN, name="x_half%d" % h) for h in range(2)]
        wy = sb.tile([P, K_PASSES * FP4_BYTES * N], U8, align_bytes=ALIGN)
        wb = sb.tile([P, N * PACK], U8, align_bytes=ALIGN)
        factor = sb.tile([P, PACK], F32, align_bytes=ALIGN)
        wa_plane = sb.tile([P, PACK * K_PASSES * P], U8, align_bytes=ALIGN)
        wa = [sb.tile([P, K_PASSES * FP4_BYTES * P], U8, align_bytes=ALIGN, name="wa%d" % j) for j in range(PACK)]
        carried = sb.tile([P, (T + 1) * PACK], F32, align_bytes=ALIGN)
        carried_rows = sb.tile([P, PACK, CARRY_ROW], F32, align_bytes=ALIGN)
        relu_rows = sb.tile([P, PACK * CHUNK], F32, align_bytes=ALIGN)
        hid = [sb.tile([P, CHUNK * PACK], BF16, align_bytes=ALIGN, name="hid%d" % c) for c in range(CHUNKS)]
        hid_codes = [sb.tile([P, CHUNK], U32, align_bytes=ALIGN, name="hid_codes%d" % c) for c in range(CHUNKS)]
        hid_plane = [sb.tile([P, CHUNK], U8, align_bytes=ALIGN, name="hid_plane%d" % c) for c in range(CHUNKS)]
        zero = sb.tile([P, PACK * P], BF16, align_bytes=ALIGN)
        zero_codes = sb.tile([P, P], U32, align_bytes=ALIGN)
        zero_plane = sb.tile([P, P], U8, align_bytes=ALIGN)

        def bank(name, index):
            return ps.tile([P, N_TILES * CHUNK], F32, name=name, tag="bank%d" % index)

        warm_bank = bank("warm_bank", 7)

        nc.vector.memset(wa_plane_raw[:].bitcast(I32), 0)
        nc.vector.memset(zero[:], 0.0)
        nc.vector.memset(x_plane[:].bitcast(I32), 0)
        nc.vector.quantize_mx(out=zero_codes[:].bitcast(FP8X4), scales=zero_plane[:], in_=zero[:])
        nc.vector.memset(wy_plane[:].bitcast(I32), 0)
        nc.vector.memset(wb_plane[:].bitcast(I32), 0)
        nc.vector.memset(carried[:, 0:PACK], 0.0)

        x_src = xt_words.rearrange("z p t b -> p z (t b)").bitcast(I32)

        def load_x(h):
            nc.sync.dma_start(
                out=x_half[h][:].bitcast(I32).rearrange("p (z t) -> p z t", z=K_PASSES),
                in_=x_src[:, :, h * HALF : (h + 1) * HALF],
            )

        load_fp4(nc, wa_raw, wa_words)
        load_scales(nc, wa_plane_raw, wa_scales)
        load_x(0)
        load_scales(nc, x_plane, xt_scales)
        nc.sync.dma_start(out=factor[:], in_=dc.rearrange("(p j) o -> p (j o)", j=PACK))
        load_x(1)
        load_scales(nc, wy_plane, wy_scales)
        load_fp4(nc, wy, wy_words)
        nc.sync.dma_start(out=wb[:].bitcast(I32), in_=wb_words[0].rearrange("p n b -> p (n b)").bitcast(I32))
        load_scales(nc, wb_plane, wb_scales)

        for w in range(WARM_PASSES):
            nc.tensor.matmul_mx(
                out=warm_bank[:, 0:P], lhsT=zero_codes[:].bitcast(FP8X4), lhsT_scale=zero_plane[:],
                rhs=zero_codes[:].bitcast(FP8X4), rhs_scale=zero_plane[:], start=True, stop=True,
            )

        for j in range(PACK):
            nc.vector.tensor_copy(
                out=wa[j][:].bitcast(U16).rearrange("p (z m) -> p z m", z=K_PASSES),
                in_=wa_raw[:].bitcast(U16).rearrange("p (z m j) -> p j z m", j=PACK, z=K_PASSES)[:, j],
            )
        for j in range(0, PACK, 2):
            nc.vector.tensor_copy(
                out=wa_plane[:].rearrange("p (j z m) -> p j z m", j=PACK, z=K_PASSES)[:, j : j + 2],
                in_=wa_plane_raw[:].rearrange("p (z m j) -> p j z m", j=PACK, z=K_PASSES)[:, j : j + 2],
            )

        def x_operand(c, z):
            h, first = divmod(c * CHUNK, HALF)
            byte = (z * HALF + first) * PACK
            column = z * T + c * CHUNK
            return x_half[h][:, byte : byte + CHUNK * PACK].bitcast(FP8X4), x_plane[:, column : column + CHUNK]

        def first_layer(c):
            a = bank("a%d" % c, c)
            for j in range(PACK):
                for z in range(K_PASSES):
                    x_codes, x_scales = x_operand(c, z)
                    column = (j * K_PASSES + z) * P
                    nc.tensor.matmul_mx(
                        out=a[:, j * CHUNK : (j + 1) * CHUNK],
                        lhsT=wa[j][:, z * FP4_BYTES * P : (z + 1) * FP4_BYTES * P].bitcast(FP4X4),
                        lhsT_scale=wa_plane[:, column : column + P],
                        rhs=x_codes, rhs_scale=x_scales,
                        start=(z == 0), stop=(z == K_PASSES - 1),
                    )
            return a

        a_bank = [first_layer(c) for c in range(CHUNKS)]

        def slots(first, count):
            return carried[:, first * PACK : (first + count) * PACK]

        def carry_on_vector(c):
            nc.vector.scalar_tensor_tensor(
                out=slots(c * CHUNK + 1, CHUNK).rearrange("p (t j) -> p t j", j=PACK),
                in0=a_bank[c][:].rearrange("p (j t) -> p t j", j=PACK), scalar=0.0,
                in1=factor[:].unsqueeze(1).broadcast_to([P, CHUNK, PACK]),
                op0=ALU.max, op1=ALU.mult,
            )

        def hidden_from_bank(c):
            nc.vector.scalar_tensor_tensor(
                out=hid[c][:].rearrange("p (t j) -> p t j", j=PACK),
                in0=a_bank[c][:].rearrange("p (j t) -> p t j", j=PACK), scalar=0.0,
                in1=slots(c * CHUNK, CHUNK).rearrange("p (t j) -> p t j", j=PACK),
                op0=ALU.max, op1=ALU.add,
            )

        def carry_on_scalar(c):
            nc.scalar.activation(out=relu_rows[:], in_=a_bank[c][:], func=ACT.Relu)
            nc.scalar.copy(out=carried_rows[:, :, 0], in_=slots(c * CHUNK, 1))
            for j in range(PACK):
                nc.scalar.activation(
                    out=carried_rows[:, j, 1 : CHUNK + 1], in_=relu_rows[:, j * CHUNK : (j + 1) * CHUNK],
                    func=ACT.Copy, scale=factor[:, j : j + 1],
                )
            nc.scalar.copy(out=slots((c + 1) * CHUNK, 1), in_=carried_rows[:, :, CHUNK])

        def hidden_from_rows(c):
            nc.vector.tensor_tensor(
                out=hid[c][:].rearrange("p (u e j) -> p u j e", e=PAIR, j=PACK),
                in0=relu_rows[:].rearrange("p (j u e) -> p u j e", e=PAIR, j=PACK),
                in1=carried_rows[:, :, 0:CHUNK].rearrange("p j (u e) -> p u j e", e=PAIR),
                op=ALU.add,
            )

        def quantize(c):
            nc.vector.quantize_mx(out=hid_codes[c][:].bitcast(FP8X4), scales=hid_plane[c][:], in_=hid[c][:])

        out_tiles = out.rearrange("(n p) t -> p n t", p=P)

        def products(c, banks):
            per_bank = N_TILES // len(banks)
            y = [bank("y%d_%d" % (c, i), index) for i, index in enumerate(banks)]
            for n in range(N_TILES):
                i, place = divmod(n, per_bank)
                for z in range(K_PASSES):
                    x_codes, x_scales = x_operand(c, z)
                    column = z * N + n * P
                    nc.tensor.matmul_mx(
                        out=y[i][:, place * CHUNK : (place + 1) * CHUNK],
                        lhsT=wy[:, FP4_BYTES * column : FP4_BYTES * (column + P)].bitcast(FP4X4),
                        lhsT_scale=wy_plane[:, column : column + P],
                        rhs=x_codes, rhs_scale=x_scales,
                        start=(place == 0 and z == 0), stop=False,
                    )
            for n in range(N_TILES):
                i, place = divmod(n, per_bank)
                nc.tensor.matmul_mx(
                    out=y[i][:, place * CHUNK : (place + 1) * CHUNK],
                    lhsT=wb[:, PACK * n * P : PACK * (n + 1) * P].bitcast(FP8X4),
                    lhsT_scale=wb_plane[:, n * P : (n + 1) * P],
                    rhs=hid_codes[c][:].bitcast(FP8X4), rhs_scale=hid_plane[c][:],
                    start=False, stop=(place == per_bank - 1),
                )
            return y

        def store(c, y, i, copy, queue):
            per_bank = N_TILES // len(y)
            result = sb.tile([P, per_bank * CHUNK], F32, align_bytes=ALIGN, name="result%d_%d" % (c, i))
            copy(out=result[:], in_=y[i][:, 0 : per_bank * CHUNK])
            queue.dma_start(
                out=out_tiles[:, i * per_bank : (i + 1) * per_bank, c * CHUNK : (c + 1) * CHUNK],
                in_=result[:].rearrange("p (n t) -> p n t", n=per_bank),
            )

        def finish_in_halves(c, banks):
            y = products(c, banks)
            for i in range(len(y)):
                store(c, y, i, nc.scalar.copy, nc.sync)

        carry_on_vector(0)
        hidden_from_bank(0)
        carry_on_scalar(SCALAR_CHUNK)
        carry_on_vector(2)
        quantize(0)
        hidden_from_rows(SCALAR_CHUNK)
        finish_in_halves(0, (4, 5))
        hidden_from_bank(2)
        quantize(1)
        finish_in_halves(1, (6, 7))
        carry_on_vector(3)
        quantize(2)
        hidden_from_bank(3)
        quantize(3)
        finish_in_halves(2, (0, 1))

        last = CHUNKS - 1
        y_last = products(last, (2, 4, 5, 6))
        for i in range(N_TILES):
            if i % 2 == 0:
                store(last, y_last, i, nc.scalar.copy, nc.scalar)
            else:
                store(last, y_last, i, nc.vector.tensor_copy, nc.sync)
